import numpy as np, ml_dtypes
CORES = [3,11,19,27,35,43]
N = 6
BF = ml_dtypes.bfloat16
def f(rng, *shape):
    return (rng.standard_normal(shape, dtype=np.float32) * np.exp2(rng.integers(-2, 3, shape[:-1] + (1,)))).astype(BF)
def wide(rng, *shape):
    v = f(rng, *shape).astype(np.float32); k = shape[:-2] + (1, shape[-1])
    return (v * np.exp2(rng.integers(-6, 7, k)) * (rng.random(k) > 0.0625)).astype(BF)
def entries(a):
    return np.ascontiguousarray(a.T).reshape(-1)
def table(e):
    return np.ascontiguousarray(np.reshape(e, (-1, 16)).T).astype(np.int32)
K, V, A, R = 2048, 6144, 2048, 384
CAP, U, HS, AS = 80, 128, 5, 2
TM = 1048576
def fine(rng, v):
    return v.astype(np.float32) * (1 + rng.random(v.shape, dtype=np.float32))
def moments(rng, uneven, *shape):
    return np.floor(np.exp2(rng.random(shape) * 20)).astype(np.int64) - 1 if uneven else rng.integers(0, TM, shape)
def owners(rng, without=-1):
    return np.stack([rng.permutation(np.repeat(np.array([q for q in range(N) if q != without]), CAP))[:R] for r in range(N)])
def full(rng):
    o = []
    for r in range(N):
        a, b = (r + 1) % N, (r + 2) % N
        rest = rng.permutation(np.repeat(np.array([q for q in range(N) if q != a and q != b]), CAP))[:R - 2 * CAP]
        o.append(rng.permutation(np.concatenate([np.repeat(np.array([a, b]), CAP), rest])))
    return np.stack(o)
def make(rng, own, key, fall=True, share=False, edge=False, low=None, uneven=False):
    tt = moments(rng, uneven, N, 8, K, HS + AS)
    if fall: tt = -np.sort(-tt, axis=3)
    if low is not None: tt = tt // 2; tt[..., :HS] += TM // 2
    h = rng.integers(0, HS + 1, (N, 8, K))
    if edge: h = HS * rng.integers(0, 2, (N, 8, K)); h[:, :, :2] = HS
    ch = rng.integers(0, K, (N, 8, K)) if share else np.zeros((N, 8, K), np.int64) + np.arange(K)
    col, s = rng.integers(0, 8, (N, R)), rng.integers(0, HS + AS, (N, R)); tie = tt[own, col, ch[own, col, key], s]; u = rng.random((N, R))
    if edge: t = np.where(u < 0.2, 0, np.where(u < 0.4, TM - 1, np.where(u < 0.7, tie, np.maximum(tie - 1, 0))))
    else: t = np.where(u < 0.25, tie, moments(rng, uneven, N, R))
    if low is not None: t = np.where(low, rng.integers(0, TM // 2, (N, R)), t)
    M = min(3 * K // 4, 2 * A // (AS + 1))
    hd = np.zeros((N, 8, K), np.int32); vt = moments(rng, uneven, N, 8, V).astype(np.int32); at = moments(rng, uneven, N, 8, A).astype(np.int32)
    vp = rng.integers(0, V + A + 1, (N, 8, V)).astype(np.int32); ap = rng.integers(0, A + 1, (N, 8, A)).astype(np.int32)
    for q in range(N):
        got = own == q; kk, tk, z = key[got], t[got], (q + 1) % N
        for c in range(8):
            x = tt[q, c]; e = np.arange(HS)[:, None] < h[q, c]; no = np.cumsum(e.reshape(-1)).reshape(HS, K) - 1; e = e & (no < V); n = np.sum(e, axis=0)
            ln = rng.integers(1, AS + 1, M)
            if edge: ln = np.where(rng.integers(0, 2, M) > 0, AS, 1); ln[:2] = AS
            e2 = np.arange(AS)[:, None] < ln; no2 = np.cumsum(e2.reshape(-1)).reshape(AS, M) - 1; e2 = e2 & (no2 < A)
            sl, sl2 = rng.permutation(V), rng.permutation(A)
            if edge:
                sl, sl2 = np.arange(V), np.arange(A); sl[1], sl[V - 1] = V - 1, 1; sl2[1], sl2[A - 1] = A - 1, 1
            m = np.where(e2, sl2[np.minimum(no2, A - 1)], A)
            want = np.array([0, 1]) if edge else rng.permutation(kk[low[got]]) if low is not None else np.zeros(0, np.int64)
            p = rng.permutation(K); o = np.concatenate([want, p[~np.isin(p, want)]])[:M]
            cont = np.full(K, A); cont[o] = m[0][np.arange(M) // 2 if share else np.arange(M)]
            ci = ch[q, c][kk]; un = ~np.any((x[ci, :HS] <= tk[:, None]) & (np.arange(HS) < n[ci][:, None]), axis=1)
            w = np.bincount(ci[un], minlength=K); most = U if low is not None else int(rng.integers(U // 2, U + 1)); tot = 0
            for j in o[w[o] > 0].tolist():
                if tot + int(w[j]) <= most: tot += int(w[j])
                else: cont[j] = A
            nx = np.where(e, sl[np.minimum(no, V - 1)], V + cont)
            hd[q, c] = nx[0][ch[q, c]]; vp[q, c][nx[e]] = np.concatenate([nx[1:], (V + cont)[None]])[e]; vt[q, c][nx[e]] = x.T[:HS][e]
            ap[z, c][m[e2]] = np.concatenate([m[1:], np.full((1, M), A)])[e2]; at[z, c][m[e2]] = x[o, HS:].T[e2]
    vv, av = (fine(rng, wide(rng, N, 8, V)), fine(rng, wide(rng, N, 8, A))) if uneven else (fine(rng, f(rng, N, 8, V)), fine(rng, f(rng, N, 8, A)))
    return {"hd": hd, "vt": vt, "vp": vp, "vv": vv, "at": at, "ap": ap, "av": av, "rk": np.stack([table(own[r] * K + key[r]) for r in range(N)]), "rt": np.stack([table(t[r]) for r in range(N)])}
def setup_inputs(rng):
    return make(rng, owners(rng), rng.integers(0, K, (N, R)))
def setup_inputs_caps(rng):
    own = full(rng); key = np.zeros((N, R), np.int64)
    for q in range(N): key[own == q] = rng.permutation(K)[:np.count_nonzero(own == q)]
    far = (own - np.arange(N)[:, None]) % N
    return make(rng, own, key, low=(far == 1) | (far == 2))
def setup_inputs_few(rng):
    own = owners(rng, int(rng.integers(0, N))); pool = np.stack([rng.permutation(K)[:16] for q in range(N)])
    return make(rng, own, pool[own, rng.integers(0, 16, (N, R))])
def setup_inputs_edge(rng):
    pool = np.stack([np.concatenate([np.array([0, 1, K - 1]), 2 + rng.permutation(K - 3)[:29]]) for q in range(N)]); own = owners(rng)
    return make(rng, own, pool[own, rng.integers(0, 32, (N, R))], edge=True)
def setup_inputs_mixed(rng):
    return make(rng, owners(rng), rng.integers(0, K, (N, R)), fall=False, share=True)
def setup_inputs_spread(rng):
    return make(rng, owners(rng), rng.integers(0, K, (N, R)), uneven=True)
def check_inputs(d):
    bad = []
    for a, top in (("hd", V + A + 1), ("vt", TM), ("vp", V + A + 1), ("at", TM), ("ap", A + 1), ("rk", N * K), ("rt", TM)):
        if np.min(d[a]) < 0 or np.max(d[a]) >= top: bad.append(a + "_range")
    for a in ("vv", "av"):
        if not np.isfinite(d[a]).all(): bad.append(a + "_finite")
    if bad: return bad
    hd, vt, vp, n = d["hd"], d["vt"], d["vp"], d["hd"].astype(np.int64); ap = np.roll(d["ap"], -1, axis=0)
    for s in range(HS): n = np.where(n < V, np.take_along_axis(vp, np.minimum(n, V - 1), 2), n)
    if (n < V).any(): bad.append("chain_in_the_heap")
    n = np.maximum(n - V, 0)
    for s in range(AS): n = np.where(n < A, np.take_along_axis(ap, np.minimum(n, A - 1), 2), n)
    if (n < A).any(): bad.append("chain_in_the_archive")
    c = np.arange(8)[:, None]; un = np.zeros((N, 8), np.int64); most = 0
    for r in range(N):
        key, t = entries(d["rk"][r]), entries(d["rt"][r]); q = key // K; most = max(most, int(np.max(np.bincount(q, minlength=N)))); n = hd[q, c, key % K]
        for s in range(HS):
            i = np.minimum(n, V - 1); n = np.where(n < V, np.where(vt[q, c, i] <= t, V + A, vp[q, c, i]), n)
        for g in range(8): un[:, g] += np.bincount(q[(n[g] >= V) & (n[g] < V + A)], minlength=N)
    if most > CAP: bad.append("reads_of_a_pair")
    if np.max(un) > U: bad.append("unfinished_walks")
    return bad
def reference(hd, vt, vp, vv, at, ap, av, rk, rt):
    y = np.zeros((N, 8, R), np.float32); c = np.arange(8)[:, None]
    for r in range(N):
        key, t = entries(rk[r]), entries(rt[r]); q = key // K; z = (q + 1) % N
        n = hd[q, c, key % K]
        for s in range(HS):
            i = np.minimum(n, V - 1); hit = (n < V) & (vt[q, c, i] <= t)
            y[r] = np.where(hit, vv[q, c, i], y[r]); n = np.where(hit, V + A, np.where(n < V, vp[q, c, i], n))
        n = n - V
        for s in range(AS):
            i = np.minimum(n, A - 1); hit = (n < A) & (at[z, c, i] <= t)
            y[r] = np.where(hit, av[z, c, i], y[r]); n = np.where(hit, A, np.where(n < A, ap[z, c, i], n))
    return {"y": y}

@@ -1,0 +1,365 @@
+from concourse.bass import DstId, RemoteDMATransfer
+from concourse.mybir import AluOpType, AxisListType, ActivationFunctionType
+
+OP = AluOpType
+COPY = ActivationFunctionType.Copy
+NR = 6
+NL, NE = 30, 480
+V, A = 6144, 2048
+BW = 6160
+BIG = 2097152.0
+SPLIT = 16
+BC, VC = 3088, 2048
+
+SHAPES = {
+    "float32": "ones_f 160 qrow 6 krow 30 imod 128 sm 36 idn 160 ide 160 ido 160 par 1 npar 1 p7 1 m8 8 gs 8 ownf 3 own5 3 pm 18 "
+               "iif 3 kf 3 keyf 3 tf 3 lh0 128 lh1 128 lh2 128 rh0 60 rh1 60 rh2 60 sb 60 vtr 384 atf 128 seed 512 aw 2056 "
+               "vw 6152 p2 2048 land 60 tl 30 tland 30 mm 30 ma 30 nh 180 gt 180 gn 180 d1 180 sc 180 rv 480 xv 480 hm 60 "
+               "x0 15 x1 15 tb 30 ra 480 xa 480 h1 30 g1 30 h2 30 p1 30 q2 30 q3 30 ans 30 am 30 hland 60 aland 30 "
+               "mask 384 maskn 384 f0 384 f1 384 ys 384",
+    "int32": "kin 3 tin 3 kidx 1 pari 1 p7i 1 owni 3 posi 3 kki 3 iii 3 keyi 3 nvp 384 nvt 384 nhd 128 nap 128 nat 128",
+    "bfloat16": "ones_b 384 tri 128 dsel 576 w1 128 sel0 384 sel1 384 sel2 384 oh 18 lb0 128 lb1 128 lb2 128 rw 24 vph 384 "
+                "vpl 384 vth 384 vtm 384 vtl 384 hdh 128 hdl 128 aph 128 apl 128 bw 6160 cw 2048 rr 2880",
+    "uint16": "ok1 24 ok2 24 ok3 24 aoff 128 areq 30 asend 30 voff 30 offs 192",
+}
+SCRATCH = {"b%d" % i: ("psum", [128, 512], "float32") for i in range(8)}
+for _d in SHAPES:
+    _w = SHAPES[_d].split()
+    for _n, _c in zip(_w[::2], _w[1::2]):
+        SCRATCH[_n] = ("sbuf", [128, int(_c)], _d)
+
+SEMAPHORES = ("sv sa st sg arr1 arrt arra arrh arry loc self1 selfh selfy yout ld_kin ld_tin ld_nvp ld_nvt ld_nhd ld_nap ld_nat "
+              "row_vph row_vpl row_vth row_vtm row_vtl row_hdh row_hdl row_aph row_apl row_atf row_av row_vv row_at2 row_av2").split()
+
+
+def rank_program(g, core, T, topo):
+    rank = T.rank_of(core)
+    if rank is None:
+        return
+    Q = {"v": g.vector, "a": g.scalar, "t": g.tensor, "g": g, "s": g.sync}
+    SN = {"v": "sv", "a": "sa", "t": "st", "g": "sg"}
+    cnt = {}
+    seen = {q: {} for q in Q}
+
+    def wait(q, toks):
+        for t in toks:
+            if t is not None and seen[q].get(t[0], 0) < t[1]:
+                Q[q].wait_ge(T.sem[t[0]], t[1])
+                seen[q][t[0]] = t[1]
+
+    def done(q, ins):
+        ins.then_inc(T.sem[SN[q]], 1)
+        cnt[SN[q]] = cnt.get(SN[q], 0) + 1
+        return (SN[q], cnt[SN[q]])
+
+    def dma(q, toks, sem, out, in_):
+        wait(q, toks)
+        Q[q].dma_start(out, in_).then_inc(T.sem[sem], 16)
+        cnt[sem] = cnt.get(sem, 0) + 16
+        return (sem, cnt[sem])
+
+    def ts(toks, out, in0, s1, op0, s2=None, op1=None):
+        wait("v", toks)
+        if op1 is None:
+            return done("v", g.vector.tensor_scalar(out, in0, s1, None, op0))
+        return done("v", g.vector.tensor_scalar(out, in0, s1, s2, op0, op1))
+
+    def tt(toks, out, a, b, op):
+        wait("v", toks)
+        return done("v", g.vector.tensor_tensor(out, a, b, op))
+
+    def cp(toks, out, in_):
+        wait("v", toks)
+        return done("v", g.vector.tensor_copy(out, in_))
+
+    def fill(out, c):
+        return done("v", g.vector.memset(out, c))
+
+    def act(toks, out, in_, scale=None):
+        wait("a", toks)
+        if scale is None:
+            return done("a", g.scalar.activation(out, in_, COPY))
+        return done("a", g.scalar.activation(out, in_, COPY, scale=scale))
+
+    def mms(toks, lst):
+        wait("t", toks)
+        for x in lst[:-1]:
+            g.tensor.matmul(*x)
+        return done("t", g.tensor.matmul(*lst[-1]))
+
+    def iota(out, pattern, base, cm):
+        return done("g", g.iota(out, pattern, base, cm, allow_small_or_imprecise_dtypes=True))
+
+    def asel(toks, out, in_, pattern, op, base, cm):
+        wait("g", toks)
+        return done("g", g.affine_select(out, in_, pattern, op, 0.0, base, cm))
+
+    cores = list(T.cores)
+    others = [cores[(rank + k) % NR] for k in range(1, NR)]
+    nxt = cores[(rank + 1) % NR]
+
+    def pick(dst, first, n):
+        return sum(1 << e for e in topo.engines(core, dst)[first:first + n])
+
+    def single(d, out, in_, sem):
+        rid, pnc = topo.addr(d)[0], topo.addr(d)[1]
+        g.remote_dma(out, in_, T.sem[sem], T.sem["loc"], pnc, rid, pick(d, 0, 8))
+        cnt["loc"] = cnt.get("loc", 0) + 8
+
+    def spread(blocks, sem):
+        tr = []
+        for k, d in enumerate(others[:4]):
+            s, o = blocks(T.rank_of(d))
+            tr.append(RemoteDMATransfer(dst_ids=[DstId(rid=topo.addr(d)[0], pnc=topo.addr(d)[1])],
+                                        dma_engine_mask=pick(d, 2 * k, 2), remote_sem=T.sem[sem], src=s, dst=o))
+        g.remote_dma_fused(tr, local_sem=T.sem["loc"])
+        cnt["loc"] = cnt.get("loc", 0) + 8
+        s, o = blocks(T.rank_of(others[4]))
+        single(others[4], o, s, sem)
+
+    ld = {}
+    for q, n, src in (("s", "kin", T.rk), ("a", "tin", T.rt), ("s", "nhd", T.hd), ("s", "nap", T.ap), ("s", "nvp", T.vp),
+                      ("s", "nvt", T.vt), ("s", "nat", T["at"])):
+        ld[n] = dma(q, [], "ld_" + n, T[n][:], src[:])
+
+    k_onesb = fill(T.ones_b[:], 1.0)
+    k_onesf = fill(T.ones_f[:], 1.0)
+    k_dz = fill(T.dsel[:], 0.0)
+    k_bwa = fill(T.bw[:, 0:BC], -BIG)
+    k_seed = fill(T.seed[:], BIG)
+    k_bwb = act([k_bwa], T.bw[:, BC:BW], T.bw[:, 0:BW - BC])
+    for x in range(0, 2056, 512):
+        k_awb = act([k_seed], T.aw[:, x:min(x + 512, 2056)], T.seed[:, 0:min(512, 2056 - x)])
+    for x in range(0, VC, 512):
+        k_vwa = act([k_seed], T.vw[:, x:x + 512], T.seed[:], 0.0)
+
+    k_q = iota(T.qrow[:], [[1, 6]], 0, 0)
+    k_tri = asel([k_onesb], T.tri[:], T.ones_b[:, 0:128], [[1, 128]], OP.is_ge, -1, -1)
+    k_kidx = done("g", g.iota(T.kidx[:], [[0, 1]], 0, 1))
+    k_kr = iota(T.krow[:], [[1, 30]], 0, 0)
+    k_im = iota(T.imod[:], [[0, 8], [1, 16]], 0, 0)
+    k = asel([k_onesf], T.sm[:], T.ones_f[:, 0:36], [[-3, 4], [-16, 9]], OP.is_ge, 0, 1)
+    k = asel([k], T.sm[:, 0:27], T.sm[:, 0:27], [[3, 3], [16, 9]], OP.is_ge, 1, -1)
+    k_sm = asel([k], T.sm[:, 27:36], T.sm[:, 27:36], [[16, 9]], OP.is_ge, 11, -1)
+
+    k_own = ts([ld["kin"]], T.owni[:], T.kin[:], 11, OP.arith_shift_right)
+    k_ownf = cp([k_own], T.ownf[:], T.owni[:])
+    for u in range(3):
+        k_oh = ts([k_ownf, k_q], T.oh[:, 6 * u:6 * u + 6], T.qrow[:], T.ownf[:, u:u + 1], OP.is_equal)
+    ml = []
+    for u in range(3):
+        o = T.b0[:, 6 * u:6 * u + 6]
+        ml.append((o, T.tri[:], T.oh[:, 6 * u:6 * u + 6], True, u == 0))
+        for w in range(u):
+            ml.append((o, T.ones_b[:, 0:128], T.oh[:, 6 * w:6 * w + 6], False, w == u - 1))
+    k_pos = mms([k_oh, k_tri, k_onesb], ml)
+    k_ki = ts([], T.keyi[:], T.kin[:], 2047, OP.bitwise_and)
+    cp([ld["tin"]], T.tf[:], T.tin[:])
+    ts([], T.own5[:], T.ownf[:], 5.0, OP.mult)
+    cp([k_ki], T.keyf[:], T.keyi[:])
+    k_pm = tt([k_pos], T.pm[:], T.b0[:, 0:18], T.oh[:], OP.mult)
+    for u in range(3):
+        wait("v", [k_pm])
+        k_po = done("v", g.vector.tensor_reduce(T.posi[:, u:u + 1], T.pm[:, 6 * u:6 * u + 6], AxisListType.X, OP.max))
+    k_ii = ts([k_po], T.iii[:], T.posi[:], 15, OP.bitwise_and)
+    k_kk = ts([], T.kki[:], T.posi[:], 4, OP.arith_shift_right)
+    k_if = cp([k_ii], T.iif[:], T.iii[:])
+    k_K = tt([k_kk], T.kf[:], T.kki[:], T.own5[:], OP.add)
+    for u in range(3):
+        ts([k_if, k_im], T["lh%d" % u][:], T.imod[:], T.iif[:, u:u + 1], OP.is_equal)
+    for u in range(3):
+        rh = T["rh%d" % u]
+        ts([k_K, k_kr], rh[:, 0:60:2], T.krow[:], T.kf[:, u:u + 1], OP.is_equal, T.keyf[:, u:u + 1], OP.mult)
+        k_rh = ts([], rh[:, 1:60:2], T.krow[:], T.kf[:, u:u + 1], OP.is_equal, T.tf[:, u:u + 1], OP.mult)
+    k_srt = mms([k_rh], [(T.b1[:, 0:60], T["lh%d" % u][:], T["rh%d" % u][:], u == 0, u == 2) for u in range(3)])
+    k_sb = cp([k_srt], T.sb[:], T.b1[:, 0:60])
+    wait("g", [k_sb])
+    spread(lambda q: (T.sb[:, 10 * q:10 * q + 10], T.land[:, 10 * rank:10 * rank + 10]), "arr1")
+    k_self1 = dma("s", [k_sb], "self1", T.land[:, 10 * rank:10 * rank + 10], T.sb[:, 10 * rank:10 * rank + 10])
+
+    rw = {}
+
+    def row(n, toks, win, p, c0, src, cols):
+        rw[n] = dma("s", toks, "row_" + n, win[p:128:16, c0:c0 + cols], src)
+
+    k = cp([ld["nat"]], T.atf[:], T.nat[:])
+    row("av", [k_awb], T.aw, 1, 0, T.av[:], A)
+    row("atf", [k], T.aw, 0, 0, T.atf[:], A)
+    k_cw = fill(T.cw[:], 0.0)
+    for n, p in (("ap", 6), ("hd", 3)):
+        nat, hi, lo = T["n" + n], T[n + "h"], T[n + "l"]
+        k = cp([ld["n" + n]], hi[:], nat[:])
+        k2 = tt([k], lo[:], nat[:], hi[:], OP.subtract)
+        row(n + "h", [k_cw, k], T.cw, p, 0, hi[:], 2048)
+        row(n + "l", [k2], T.cw, p + 1, 0, lo[:], 2048)
+    k = cp([ld["nvp"]], T.vph[:], T.nvp[:])
+    k2 = tt([k], T.vpl[:], T.nvp[:], T.vph[:], OP.subtract)
+    row("vph", [k_bwb, k], T.bw, 0, 8, T.vph[:], V)
+    row("vpl", [k2], T.bw, 1, 8, T.vpl[:], V)
+    k = cp([ld["nvt"]], T.vth[:], T.nvt[:])
+    k2 = tt([k], T.vtr[:], T.nvt[:], T.vth[:], OP.subtract)
+    k3 = cp([k2], T.vtm[:], T.vtr[:])
+    k4 = tt([k3], T.vtl[:], T.vtr[:], T.vtm[:], OP.subtract)
+    row("vth", [k], T.bw, 9, 8, T.vth[:], V)
+    row("vtm", [k3], T.bw, 10, 8, T.vtm[:], V)
+    row("vtl", [k4], T.bw, 11, 8, T.vtl[:], V)
+    k_d = cp([k_sm, k_dz], T.dsel[:, 15:576:16], T.sm[:])
+    heap_rows = [rw[n] for n in ("vph", "vpl", "vth", "vtm", "vtl")]
+    cw_rows = [rw[n] for n in ("aph", "apl", "hdh", "hdl")]
+
+    def wrap(toks, field, out, src):
+        x = 144 * field + 15
+        return mms(toks, [(out, T.dsel[:, x - r:x - r + 128], src(r), r == 0, r == 15) for r in range(16)])
+
+    k_apw = wrap([k_d] + cw_rows, 2, T.b6[:, 0:128], lambda r: T.cw[:, r:2048:16])
+    k_ao = cp([k_apw], T.aoff[:], T.b6[:, 0:128])
+    k_p2 = act([k_ao, rw["av"], rw["atf"]], T.p2[:], T.aw[:, 0:2056].indirect(T.aoff[:, 0:128]))
+    row("at2", [k_p2], T.aw, 2, 0, T.p2[0:128:16, :], A)
+    row("av2", [k_p2], T.aw, 3, 0, T.p2[1:128:16, :], A)
+
+    k_vwb = iota(T.vw[:, VC:6152], [[0, 6152 - VC]], 0, 0)
+    row("vv", [k_vwa, k_vwb], T.vw, 0, 0, T.vv[:], V)
+    k_idn = asel([k_onesf], T.idn[:], T.ones_f[:], [[1, 160]], OP.is_equal, -16, -1)
+    k = asel([k_onesb], T.w1[:], T.ones_b[:, 0:128], [[0, 8], [-8, 16]], OP.is_ge, 0, 1)
+    k_w1 = asel([k], T.w1[:], T.w1[:], [[0, 8], [8, 16]], OP.is_ge, 7, -1)
+    k = asel([k_onesf], T.gs[:], T.ones_f[:, 0:8], [[-16, 8]], OP.is_ge, 0, 1)
+    k_gs = asel([k], T.gs[:], T.gs[:], [[16, 8]], OP.is_ge, 15, -1)
+
+    k = ts([k_kidx], T.pari[:], T.kidx[:], 4, OP.arith_shift_right, 1, OP.bitwise_and)
+    k2 = ts([], T.p7i[:], T.kidx[:], 7, OP.bitwise_and)
+    k_par = cp([k], T.par[:], T.pari[:])
+    k = cp([k2], T.p7[:], T.p7i[:])
+    k_np = ts([k_par], T.npar[:], T.par[:], -1.0, OP.mult, 1.0, OP.add)
+    k_m8 = ts([k], T.m8[:], T.krow[:, 0:8], T.p7[:], OP.is_equal)
+    k_gt0 = fill(T.gt[:], 0.0)
+
+    EV = 16 * SPLIT
+
+    def gather(win, toks, off, r, x0):
+        kb = act(toks, r[:, x0 + EV:x0 + NE], win.indirect(off(SPLIT, NL)))
+        wait("v", toks)
+        return done("v", g.vector.tensor_copy(r[:, x0:x0 + EV], win.indirect(off(0, SPLIT)))), kb
+
+    k_off = cp([("arr1", 16), k_self1], T.offs[:, 0:30], T.land[:, 0:60:2])
+    tread = T.land[:, 1:60:2]
+    rtok, nread, vread, ntok, vtok = {}, {}, {}, {}, {}
+    rtok[0] = gather(T.cw[:, 0:2048], [k_off] + cw_rows, lambda a, b: T.offs[:, a:b], T.rr, 0)
+    k_tl = cp([], T.tl[:], tread)
+    wait("g", [k_tl])
+    single(nxt, T.tland[:], T.tl[:], "arrt")
+
+    nbank = {s: T.b2 if s % 2 else T.b3 for s in range(1, 7)}
+    vbank = {s: T.b4 if s % 2 else T.b5 for s in range(1, 6)}
+
+    def nwrap(s):
+        ntok[s] = wrap(list(rtok[s - 1]) + [nread.get(s - 2)], 1 if s == 1 else 0, nbank[s][:, 0:30],
+                       lambda r: T.rr[:, NE * (s - 1) + r:NE * s:16])
+
+    def vwrap(s):
+        vtok[s] = wrap(list(rtok[s]) + [vread.get(s - 2)], 3, vbank[s][:, 0:30], lambda r: T.rr[:, NE * s + r:NE * (s + 1):16])
+
+    def later(s):
+        vread[s] = tt([vtok[s], k_gt0], T.gt[:, 6 - s:180:6], vbank[s][:, 0:30], tread, OP.is_gt)
+
+    for s in range(1, 7):
+        nwrap(s)
+        if s in (3, 4, 5):
+            vwrap(s - 2)
+        if s == 4:
+            k_okp = mms([k_rw, k_w1], [(T.b7[:, 0:24], T.w1[:], T.rw[:], True, True)])
+        n = nbank[s][:, 0:30]
+        if s == 6:
+            break
+        x = 32 * s
+        k_off = ts([ntok[s]], T.offs[:, x:x + 30], n, 8.0, OP.add, float(V + 8), OP.min)
+        rtok[s] = gather(T.bw[:], [k_off] + heap_rows, lambda a, b: T.offs[:, x + a:x + b], T.rr, NE * s)
+        cp([], T.nh[:, 6 - s:180:6], n)
+        k_mm = cp([], T.mm[:], n) if s == 1 else tt([k_mm], T.mm[:], T.mm[:], n, OP.max)
+        nread[s] = k_mm
+        for u in range(3):
+            if s == 1:
+                k_rw = ts([k_m8], T.rw[:, u:24:3], T.m8[:], T.kf[:, u:u + 1], OP.mult)
+            if s == (2, 2, 3)[u]:
+                k_lb = cp([], T["lb%d" % u][:], T["lh%d" % u][:])
+        if s > 3:
+            later(s - 3)
+    k_ma = tt([ntok[6], k_mm], T.ma[:], n, T.mm[:], OP.max)
+    k_as = ts([k_ma], T.asend[:], T.ma[:], float(-V), OP.add)
+    wait("g", [k_as])
+    single(nxt, T.areq[:], T.asend[:], "arra")
+    k_nh = cp([], T.nh[:, 0:180:6], n)
+
+    vwrap(4)
+    later(3)
+    vwrap(5)
+    k_ide = ts([k_idn, k_np], T.ide[:], T.idn[:], T.npar[:], OP.mult)
+    k_ido = ts([], T.ido[:], T.idn[:], T.par[:], OP.mult)
+    for o, m, b in (("ok1", 1.0, 0.0), ("ok2", 2.0, 0.0), ("ok3", 2.0, 1.0)):
+        k_ok = ts([k_okp], T[o][:], T.b7[:, 0:24], m, OP.mult, b, OP.add)
+    later(4)
+    later(5)
+    k = tt([vread[5], k_nh], T.gn[:], T.gt[:], T.nh[:], OP.mult)
+    k = tt([k], T.d1[:], T.nh[:], T.gn[:], OP.subtract)
+    wait("v", [k])
+    k_sc = done("v", g.vector.tensor_tensor_scan(T.sc[:], T.gt[:], T.d1[:], 0.0, OP.mult, OP.add))
+    k_vo = ts([k_sc], T.voff[:], T.sc[:, 5:180:6], float(V), OP.min)
+    k_nf = ts([], T.hm[:, 1:60:2], T.sc[:, 5:180:6], float(V), OP.is_ge)
+
+    def turn(toks, src, dst):
+        wait("v", toks[:1])
+        done("v", g.vector.transpose(dst[:, 0:EV], src[:, 0:EV]))
+        wait("v", toks[1:])
+        return done("v", g.vector.transpose(dst[:, EV:NE], src[:, EV:NE]))
+
+    def swap(toks, out, src):
+        ml = []
+        for e in range(2):
+            for h in range(2):
+                x = 16 + 16 * (e - h)
+                ml.append((out[:, e:30:2], (T.ido if e else T.ide)[:, x:x + 128], src(h), h == 0, h == 1))
+        return mms(toks, ml)
+
+    k_rv = gather(T.vw[:], [k_vo, rw["vv"]], lambda a, b: T.voff[:, a:b], T.rv, 0)
+    k_xv = turn(k_rv, T.rv, T.xv)
+    k_pv = swap([k_xv, k_ide, k_ido, k_ao], T.b6[:, 0:30], lambda h: T.xv[:, 16 * h:NE:32])
+    ts([("arrt", 8), k_np], T.x0[:], T.tland[:, 0:30:2], T.npar[:], OP.mult)
+    k = ts([], T.x1[:], T.tland[:, 1:30:2], T.par[:], OP.mult)
+    tt([k], T.tb[:, 0:30:2], T.x0[:], T.x1[:], OP.add)
+    k_tb = tt([], T.tb[:, 1:30:2], T.x0[:], T.x1[:], OP.add)
+    k_hm = cp([k_pv], T.hm[:, 0:60:2], T.b6[:, 0:30])
+    wait("g", [k_hm])
+    spread(lambda r: (T.hm[:, 10 * r:10 * r + 10], T.hland[:, 10 * rank:10 * rank + 10]), "arrh")
+    k_selfh = dma("s", [k_hm], "selfh", T.hland[:, 10 * rank:10 * rank + 10], T.hm[:, 10 * rank:10 * rank + 10])
+    for u in range(3):
+        k_sel = asel([k_onesb], T["sel%d" % u][:], T.ones_b[:], [[-1, 8], [1000, 3], [-8, 16]], OP.is_equal, -1000 * u, 1)
+
+    own = (rank - 1) % NR
+    k_ra = gather(T.aw[:, 0:2056], [("arra", 8), rw["at2"], rw["av2"]], lambda a, b: T.areq[:, a:b], T.ra, 0)
+    k_xa = turn(k_ra, T.ra, T.xa)
+    t1, v1, t2, v2 = (T.xa[:, j:NE:16] for j in range(4))
+    k_h2 = tt([k_xa, k_tb], T.h2[:], t2, T.tb[:], OP.is_le)
+    k_g1 = tt([], T.g1[:], t1, T.tb[:], OP.is_gt)
+    k_h1 = tt([], T.h1[:], t1, T.tb[:], OP.is_le)
+    k_q2 = tt([k_h2], T.q2[:], T.h2[:], v2, OP.mult)
+    k_p1 = tt([k_h1], T.p1[:], T.h1[:], v1, OP.mult)
+    k_q3 = tt([k_q2, k_g1], T.q3[:], T.q2[:], T.g1[:], OP.mult)
+    k_ans = tt([k_q3, k_p1], T.ans[:], T.q3[:], T.p1[:], OP.add)
+    k_pa = swap([k_ans], T.b2[:, 0:30], lambda h: T.ans[:, h:30:2])
+    k_am = cp([k_pa], T.am[:], T.b2[:, 0:30])
+    wait("g", [k_am])
+    spread(lambda r: (T.am[:, 5 * r:5 * r + 5], T.aland[:, 5 * own:5 * own + 5]), "arry")
+    k_selfy = dma("s", [k_am], "selfy", T.aland[:, 5 * own:5 * own + 5], T.am[:, 5 * rank:5 * rank + 5])
+
+    k_mk = mms([k_lb, k_sel, k_ok], [(T.b7[:, 0:384], T["lb%d" % u][:], T["sel%d" % u][:], u == 0, u == 2) for u in range(3)])
+    k_mask = cp([k_mk], T.mask[:], T.b7[:, 0:384])
+    k_f0 = tt([k_mask, k_ok, ("arrh", 16), k_selfh], T.f0[:], T.hland[:].indirect(T.ok2[:]), T.mask[:], OP.mult)
+    k_mn = tt([], T.maskn[:], T.hland[:].indirect(T.ok3[:]), T.mask[:], OP.mult)
+    Y = T.b0[0:8, 0:384]
+    mms([k_f0, k_gs, k_pm], [(Y, T.gs[:], T.f0[:], True, False)])
+    k_f1 = tt([k_mn, ("arry", 16), k_selfy], T.f1[:], T.aland[:].indirect(T.ok1[:]), T.maskn[:], OP.mult)
+    k_y = mms([k_f1], [(Y, T.gs[:], T.f1[:], False, True)])
+    k_ys = cp([k_y], T.ys[0:8, :], Y)
+    dma("s", [k_ys], "yout", T.y[:], T.ys[0:8, :])
+
+    cnt.update({"arr1": 16, "arrt": 8, "arra": 8, "arrh": 16, "arry": 16})
+    wait("g", [(n, cnt[n]) for n in SEMAPHORES])

@@ -9,12 +9,12 @@ V, A = 6144, 2048
 BW = 6160
 BIG = 2097152.0
 SPLIT = 16
-BC, VC = 3088, 2048
+BC, VC = 2576, 2048
 
 SHAPES = {
     "float32": "ones_f 160 qrow 6 krow 30 imod 128 sm 36 idn 160 ide 160 ido 160 par 1 npar 1 p7 1 m8 8 gs 8 ownf 3 own5 3 pm 18 "
                "iif 3 kf 3 keyf 3 tf 3 lh0 128 lh1 128 lh2 128 rh0 60 rh1 60 rh2 60 sb 60 vtr 384 atf 128 seed 512 aw 2056 "
-               "vw 6152 p2 2048 land 60 tl 30 tland 30 mm 30 ma 30 nh 180 gt 180 gn 180 d1 180 sc 180 rv 480 xv 480 hm 60 "
+               "vw 6152 p2 2048 land 60 tl 30 tland 30 mm 30 ma 30 nh 180 gt 180 hit 180 d1 180 sc 180 rv 480 xv 480 hm 60 "
                "x0 15 x1 15 tb 30 ra 480 xa 480 h1 30 g1 30 h2 30 p1 30 q2 30 q3 30 ans 30 am 30 hland 60 aland 30 "
                "mask 384 maskn 384 f0 384 f1 384 ys 384",
     "int32": "kin 3 tin 3 kidx 1 pari 1 p7i 1 owni 3 posi 3 kki 3 iii 3 keyi 3 nvp 384 nvt 384 nhd 128 nap 128 nat 128",
@@ -28,8 +28,9 @@ for _d in SHAPES:
     for _n, _c in zip(_w[::2], _w[1::2]):
         SCRATCH[_n] = ("sbuf", [128, int(_c)], _d)
 
-SEMAPHORES = ("sv sa st sg arr1 arrt arra arrh arry loc self1 selfh selfy yout ld_kin ld_tin ld_nvp ld_nvt ld_nhd ld_nap ld_nat "
-              "row_vph row_vpl row_vth row_vtm row_vtl row_hdh row_hdl row_aph row_apl row_atf row_av row_vv row_at2 row_av2").split()
+SEMAPHORES = ("sv sa st sg arr1 arrt arra arrh arry loc self1 selfh selfy y0 y1 y2 ld_kin ld_tin ld_nvp ld_nvt ld_nhd ld_nap "
+              "ld_nat row_vph row_vpl row_vth row_vtm row_vtl row_hdh row_hdl row_aph row_apl row_atf row_av row_vv row_at2 "
+              "row_av2").split()
 
 
 def rank_program(g, core, T, topo):
@@ -118,29 +119,36 @@ def rank_program(g, core, T, topo):
         single(others[4], o, s, sem)
 
     ld = {}
-    for q, n, src in (("s", "kin", T.rk), ("a", "tin", T.rt), ("s", "nhd", T.hd), ("s", "nap", T.ap), ("s", "nvp", T.vp),
+    for q, n, src in (("s", "kin", T.rk), ("a", "tin", T.rt), ("s", "nap", T.ap), ("s", "nhd", T.hd), ("s", "nvp", T.vp),
                       ("s", "nvt", T.vt), ("s", "nat", T["at"])):
         ld[n] = dma(q, [], "ld_" + n, T[n][:], src[:])
 
-    k_onesb = fill(T.ones_b[:], 1.0)
-    k_onesf = fill(T.ones_f[:], 1.0)
-    k_dz = fill(T.dsel[:], 0.0)
-    k_bwa = fill(T.bw[:, 0:BC], -BIG)
     k_seed = fill(T.seed[:], BIG)
-    k_bwb = act([k_bwa], T.bw[:, BC:BW], T.bw[:, 0:BW - BC])
-    for x in range(0, 2056, 512):
-        k_awb = act([k_seed], T.aw[:, x:min(x + 512, 2056)], T.seed[:, 0:min(512, 2056 - x)])
-    for x in range(0, VC, 512):
-        k_vwa = act([k_seed], T.vw[:, x:x + 512], T.seed[:], 0.0)
+    k_onesb = fill(T.ones_b[:, 0:128], 1.0)
+    k_onesf = fill(T.ones_f[:], 1.0)
+    k_bwa = fill(T.bw[:, 0:BC], -BIG)
+
+    def seed(win, c0, c1, scale=None):
+        for x in range(c0, c1, 512):
+            n = min(512, c1 - x)
+            k = act([k_seed], win[:, x:x + n], T.seed[:, 0:n], scale)
+        return k
+
+    k_cw = seed(T.cw, 0, 2048, 0.0)
+    k_bwb = seed(T.bw, BC, BW, -1.0)
+    k_aw = seed(T.aw, 0, 2056)
+    k_vwa = seed(T.vw, 0, VC, 0.0)
 
     k_q = iota(T.qrow[:], [[1, 6]], 0, 0)
     k_tri = asel([k_onesb], T.tri[:], T.ones_b[:, 0:128], [[1, 128]], OP.is_ge, -1, -1)
-    k_kidx = done("g", g.iota(T.kidx[:], [[0, 1]], 0, 1))
     k_kr = iota(T.krow[:], [[1, 30]], 0, 0)
     k_im = iota(T.imod[:], [[0, 8], [1, 16]], 0, 0)
+    k_kidx = done("g", g.iota(T.kidx[:], [[0, 1]], 0, 1))
     k = asel([k_onesf], T.sm[:], T.ones_f[:, 0:36], [[-3, 4], [-16, 9]], OP.is_ge, 0, 1)
     k = asel([k], T.sm[:, 0:27], T.sm[:, 0:27], [[3, 3], [16, 9]], OP.is_ge, 1, -1)
     k_sm = asel([k], T.sm[:, 27:36], T.sm[:, 27:36], [[16, 9]], OP.is_ge, 11, -1)
+    k = asel([k_onesf], T.gs[:], T.ones_f[:, 0:8], [[-16, 8]], OP.is_ge, 0, 1)
+    k_gs = asel([k], T.gs[:], T.gs[:], [[16, 8]], OP.is_ge, 15, -1)
 
     k_own = ts([ld["kin"]], T.owni[:], T.kin[:], 11, OP.arith_shift_right)
     k_ownf = cp([k_own], T.ownf[:], T.owni[:])
@@ -166,12 +174,11 @@ def rank_program(g, core, T, topo):
     k_if = cp([k_ii], T.iif[:], T.iii[:])
     k_K = tt([k_kk], T.kf[:], T.kki[:], T.own5[:], OP.add)
     for u in range(3):
-        ts([k_if, k_im], T["lh%d" % u][:], T.imod[:], T.iif[:, u:u + 1], OP.is_equal)
-    for u in range(3):
-        rh = T["rh%d" % u]
+        lh, rh = T["lh%d" % u], T["rh%d" % u]
+        ts([k_if, k_im], lh[:], T.imod[:], T.iif[:, u:u + 1], OP.is_equal)
         ts([k_K, k_kr], rh[:, 0:60:2], T.krow[:], T.kf[:, u:u + 1], OP.is_equal, T.keyf[:, u:u + 1], OP.mult)
         k_rh = ts([], rh[:, 1:60:2], T.krow[:], T.kf[:, u:u + 1], OP.is_equal, T.tf[:, u:u + 1], OP.mult)
-    k_srt = mms([k_rh], [(T.b1[:, 0:60], T["lh%d" % u][:], T["rh%d" % u][:], u == 0, u == 2) for u in range(3)])
+        k_srt = mms([k_rh], [(T.b1[:, 0:60], lh[:], rh[:], u == 0, u == 2)])
     k_sb = cp([k_srt], T.sb[:], T.b1[:, 0:60])
     wait("g", [k_sb])
     spread(lambda q: (T.sb[:, 10 * q:10 * q + 10], T.land[:, 10 * rank:10 * rank + 10]), "arr1")
@@ -182,10 +189,6 @@ def rank_program(g, core, T, topo):
     def row(n, toks, win, p, c0, src, cols):
         rw[n] = dma("s", toks, "row_" + n, win[p:128:16, c0:c0 + cols], src)
 
-    k = cp([ld["nat"]], T.atf[:], T.nat[:])
-    row("av", [k_awb], T.aw, 1, 0, T.av[:], A)
-    row("atf", [k], T.aw, 0, 0, T.atf[:], A)
-    k_cw = fill(T.cw[:], 0.0)
     for n, p in (("ap", 6), ("hd", 3)):
         nat, hi, lo = T["n" + n], T[n + "h"], T[n + "l"]
         k = cp([ld["n" + n]], hi[:], nat[:])
@@ -196,14 +199,18 @@ def rank_program(g, core, T, topo):
     k2 = tt([k], T.vpl[:], T.nvp[:], T.vph[:], OP.subtract)
     row("vph", [k_bwb, k], T.bw, 0, 8, T.vph[:], V)
     row("vpl", [k2], T.bw, 1, 8, T.vpl[:], V)
+    k_dz = fill(T.dsel[:], 0.0)
     k = cp([ld["nvt"]], T.vth[:], T.nvt[:])
     k2 = tt([k], T.vtr[:], T.nvt[:], T.vth[:], OP.subtract)
+    k_d = cp([k_sm, k_dz], T.dsel[:, 15:576:16], T.sm[:])
     k3 = cp([k2], T.vtm[:], T.vtr[:])
     k4 = tt([k3], T.vtl[:], T.vtr[:], T.vtm[:], OP.subtract)
     row("vth", [k], T.bw, 9, 8, T.vth[:], V)
     row("vtm", [k3], T.bw, 10, 8, T.vtm[:], V)
     row("vtl", [k4], T.bw, 11, 8, T.vtl[:], V)
-    k_d = cp([k_sm, k_dz], T.dsel[:, 15:576:16], T.sm[:])
+    k = cp([ld["nat"]], T.atf[:], T.nat[:])
+    row("av", [k_aw], T.aw, 1, 0, T.av[:], A)
+    row("atf", [k], T.aw, 0, 0, T.atf[:], A)
     heap_rows = [rw[n] for n in ("vph", "vpl", "vth", "vtm", "vtl")]
     cw_rows = [rw[n] for n in ("aph", "apl", "hdh", "hdl")]
 
@@ -212,26 +219,17 @@ def rank_program(g, core, T, topo):
         return mms(toks, [(out, T.dsel[:, x - r:x - r + 128], src(r), r == 0, r == 15) for r in range(16)])
 
     k_apw = wrap([k_d] + cw_rows, 2, T.b6[:, 0:128], lambda r: T.cw[:, r:2048:16])
-    k_ao = cp([k_apw], T.aoff[:], T.b6[:, 0:128])
-    k_p2 = act([k_ao, rw["av"], rw["atf"]], T.p2[:], T.aw[:, 0:2056].indirect(T.aoff[:, 0:128]))
-    row("at2", [k_p2], T.aw, 2, 0, T.p2[0:128:16, :], A)
-    row("av2", [k_p2], T.aw, 3, 0, T.p2[1:128:16, :], A)
 
     k_vwb = iota(T.vw[:, VC:6152], [[0, 6152 - VC]], 0, 0)
-    row("vv", [k_vwa, k_vwb], T.vw, 0, 0, T.vv[:], V)
-    k_idn = asel([k_onesf], T.idn[:], T.ones_f[:], [[1, 160]], OP.is_equal, -16, -1)
     k = asel([k_onesb], T.w1[:], T.ones_b[:, 0:128], [[0, 8], [-8, 16]], OP.is_ge, 0, 1)
     k_w1 = asel([k], T.w1[:], T.w1[:], [[0, 8], [8, 16]], OP.is_ge, 7, -1)
-    k = asel([k_onesf], T.gs[:], T.ones_f[:, 0:8], [[-16, 8]], OP.is_ge, 0, 1)
-    k_gs = asel([k], T.gs[:], T.gs[:], [[16, 8]], OP.is_ge, 15, -1)
+    k_idn = asel([k_onesf], T.idn[:], T.ones_f[:], [[1, 160]], OP.is_equal, -16, -1)
 
     k = ts([k_kidx], T.pari[:], T.kidx[:], 4, OP.arith_shift_right, 1, OP.bitwise_and)
     k2 = ts([], T.p7i[:], T.kidx[:], 7, OP.bitwise_and)
     k_par = cp([k], T.par[:], T.pari[:])
-    k = cp([k2], T.p7[:], T.p7i[:])
-    k_np = ts([k_par], T.npar[:], T.par[:], -1.0, OP.mult, 1.0, OP.add)
-    k_m8 = ts([k], T.m8[:], T.krow[:, 0:8], T.p7[:], OP.is_equal)
-    k_gt0 = fill(T.gt[:], 0.0)
+    k_p7 = cp([k2], T.p7[:], T.p7i[:])
+    k_ao = cp([k_apw], T.aoff[:], T.b6[:, 0:128])
 
     EV = 16 * SPLIT
 
@@ -240,70 +238,74 @@ def rank_program(g, core, T, topo):
         wait("v", toks)
         return done("v", g.vector.tensor_copy(r[:, x0:x0 + EV], win.indirect(off(0, SPLIT)))), kb
 
+    def follow(x):
+        a, b = 26 * x, min(26 * x + 26, 128)
+        return act([k_ao, rw["av"], rw["atf"]], T.p2[:, 16 * a:16 * b], T.aw[:, 0:2056].indirect(T.aoff[:, a:b]))
+
     k_off = cp([("arr1", 16), k_self1], T.offs[:, 0:30], T.land[:, 0:60:2])
     tread = T.land[:, 1:60:2]
     rtok, nread, vread, ntok, vtok = {}, {}, {}, {}, {}
     rtok[0] = gather(T.cw[:, 0:2048], [k_off] + cw_rows, lambda a, b: T.offs[:, a:b], T.rr, 0)
+    follow(0)
     k_tl = cp([], T.tl[:], tread)
+    k_np = ts([k_par], T.npar[:], T.par[:], -1.0, OP.mult, 1.0, OP.add)
+    k_m8 = ts([k_p7], T.m8[:], T.krow[:, 0:8], T.p7[:], OP.is_equal)
+    fill(T.gt[:], 0.0)
+    k_gt0 = fill(T.ones_b[:, 128:384], 1.0)
     wait("g", [k_tl])
     single(nxt, T.tland[:], T.tl[:], "arrt")
 
     nbank = {s: T.b2 if s % 2 else T.b3 for s in range(1, 7)}
     vbank = {s: T.b4 if s % 2 else T.b5 for s in range(1, 6)}
 
-    def nwrap(s):
-        ntok[s] = wrap(list(rtok[s - 1]) + [nread.get(s - 2)], 1 if s == 1 else 0, nbank[s][:, 0:30],
-                       lambda r: T.rr[:, NE * (s - 1) + r:NE * s:16])
-
-    def vwrap(s):
-        vtok[s] = wrap(list(rtok[s]) + [vread.get(s - 2)], 3, vbank[s][:, 0:30], lambda r: T.rr[:, NE * s + r:NE * (s + 1):16])
-
     def later(s):
-        vread[s] = tt([vtok[s], k_gt0], T.gt[:, 6 - s:180:6], vbank[s][:, 0:30], tread, OP.is_gt)
+        x = slice(6 - s, 180, 6)
+        k = tt([vtok[s], k_gt0], T.hit[:, x], vbank[s][:, 0:30], tread, OP.is_le)
+        vread[s] = tt([], T.gt[:, x], vbank[s][:, 0:30], tread, OP.is_gt)
+        return tt([k], T.d1[:, x], T.hit[:, x], T.nh[:, x], OP.mult)
 
     for s in range(1, 7):
-        nwrap(s)
-        if s in (3, 4, 5):
-            vwrap(s - 2)
-        if s == 4:
-            k_okp = mms([k_rw, k_w1], [(T.b7[:, 0:24], T.w1[:], T.rw[:], True, True)])
+        ntok[s] = wrap(list(rtok[s - 1]) + [nread.get(s - 2)], 1 if s == 1 else 0, nbank[s][:, 0:30],
+                       lambda r: T.rr[:, NE * (s - 1) + r:NE * s:16])
+        if s > 1:
+            vtok[s - 1] = wrap([vread.get(s - 3)], 3, vbank[s - 1][:, 0:30], lambda r: T.rr[:, NE * (s - 1) + r:NE * s:16])
         n = nbank[s][:, 0:30]
         if s == 6:
             break
         x = 32 * s
         k_off = ts([ntok[s]], T.offs[:, x:x + 30], n, 8.0, OP.add, float(V + 8), OP.min)
         rtok[s] = gather(T.bw[:], [k_off] + heap_rows, lambda a, b: T.offs[:, x + a:x + b], T.rr, NE * s)
+        if s < 5:
+            k_p2 = follow(s)
         cp([], T.nh[:, 6 - s:180:6], n)
         k_mm = cp([], T.mm[:], n) if s == 1 else tt([k_mm], T.mm[:], T.mm[:], n, OP.max)
         nread[s] = k_mm
         for u in range(3):
             if s == 1:
                 k_rw = ts([k_m8], T.rw[:, u:24:3], T.m8[:], T.kf[:, u:u + 1], OP.mult)
-            if s == (2, 2, 3)[u]:
+            if s == 2:
                 k_lb = cp([], T["lb%d" % u][:], T["lh%d" % u][:])
-        if s > 3:
-            later(s - 3)
+        if s > 2:
+            later(s - 2)
     k_ma = tt([ntok[6], k_mm], T.ma[:], n, T.mm[:], OP.max)
     k_as = ts([k_ma], T.asend[:], T.ma[:], float(-V), OP.add)
     wait("g", [k_as])
     single(nxt, T.areq[:], T.asend[:], "arra")
-    k_nh = cp([], T.nh[:, 0:180:6], n)
+    for u in range(3):
+        k_sel = asel([k_gt0], T["sel%d" % u][:], T.ones_b[:], [[-1, 8], [1000, 3], [-8, 16]], OP.is_equal, -1000 * u, 1)
+    row("vv", [k_vwa, k_vwb], T.vw, 0, 0, T.vv[:], V)
+    row("at2", [k_p2], T.aw, 2, 0, T.p2[0:128:16, :], A)
+    row("av2", [k_p2], T.aw, 3, 0, T.p2[1:128:16, :], A)
 
-    vwrap(4)
-    later(3)
-    vwrap(5)
+    cp([], T.d1[:, 0:180:6], n)
+    later(4)
     k_ide = ts([k_idn, k_np], T.ide[:], T.idn[:], T.npar[:], OP.mult)
     k_ido = ts([], T.ido[:], T.idn[:], T.par[:], OP.mult)
-    for o, m, b in (("ok1", 1.0, 0.0), ("ok2", 2.0, 0.0), ("ok3", 2.0, 1.0)):
-        k_ok = ts([k_okp], T[o][:], T.b7[:, 0:24], m, OP.mult, b, OP.add)
-    later(4)
-    later(5)
-    k = tt([vread[5], k_nh], T.gn[:], T.gt[:], T.nh[:], OP.mult)
-    k = tt([k], T.d1[:], T.nh[:], T.gn[:], OP.subtract)
+    k_okp = mms([k_rw, k_w1], [(T.b7[:, 0:24], T.w1[:], T.rw[:], True, True)])
+    k = later(5)
     wait("v", [k])
     k_sc = done("v", g.vector.tensor_tensor_scan(T.sc[:], T.gt[:], T.d1[:], 0.0, OP.mult, OP.add))
     k_vo = ts([k_sc], T.voff[:], T.sc[:, 5:180:6], float(V), OP.min)
-    k_nf = ts([], T.hm[:, 1:60:2], T.sc[:, 5:180:6], float(V), OP.is_ge)
 
     def turn(toks, src, dst):
         wait("v", toks[:1])
@@ -322,19 +324,18 @@ def rank_program(g, core, T, topo):
     k_rv = gather(T.vw[:], [k_vo, rw["vv"]], lambda a, b: T.voff[:, a:b], T.rv, 0)
     k_xv = turn(k_rv, T.rv, T.xv)
     k_pv = swap([k_xv, k_ide, k_ido, k_ao], T.b6[:, 0:30], lambda h: T.xv[:, 16 * h:NE:32])
+    k_nf = ts([], T.hm[:, 1:60:2], T.sc[:, 5:180:6], float(V), OP.is_ge)
     ts([("arrt", 8), k_np], T.x0[:], T.tland[:, 0:30:2], T.npar[:], OP.mult)
     k = ts([], T.x1[:], T.tland[:, 1:30:2], T.par[:], OP.mult)
     tt([k], T.tb[:, 0:30:2], T.x0[:], T.x1[:], OP.add)
     k_tb = tt([], T.tb[:, 1:30:2], T.x0[:], T.x1[:], OP.add)
+
+    own = (rank - 1) % NR
+    k_ra = gather(T.aw[:, 0:2056], [("arra", 8), rw["at2"], rw["av2"]], lambda a, b: T.areq[:, a:b], T.ra, 0)
     k_hm = cp([k_pv], T.hm[:, 0:60:2], T.b6[:, 0:30])
     wait("g", [k_hm])
     spread(lambda r: (T.hm[:, 10 * r:10 * r + 10], T.hland[:, 10 * rank:10 * rank + 10]), "arrh")
     k_selfh = dma("s", [k_hm], "selfh", T.hland[:, 10 * rank:10 * rank + 10], T.hm[:, 10 * rank:10 * rank + 10])
-    for u in range(3):
-        k_sel = asel([k_onesb], T["sel%d" % u][:], T.ones_b[:], [[-1, 8], [1000, 3], [-8, 16]], OP.is_equal, -1000 * u, 1)
-
-    own = (rank - 1) % NR
-    k_ra = gather(T.aw[:, 0:2056], [("arra", 8), rw["at2"], rw["av2"]], lambda a, b: T.areq[:, a:b], T.ra, 0)
     k_xa = turn(k_ra, T.ra, T.xa)
     t1, v1, t2, v2 = (T.xa[:, j:NE:16] for j in range(4))
     k_h2 = tt([k_xa, k_tb], T.h2[:], t2, T.tb[:], OP.is_le)
@@ -345,6 +346,8 @@ def rank_program(g, core, T, topo):
     k_q3 = tt([k_q2, k_g1], T.q3[:], T.q2[:], T.g1[:], OP.mult)
     k_ans = tt([k_q3, k_p1], T.ans[:], T.q3[:], T.p1[:], OP.add)
     k_pa = swap([k_ans], T.b2[:, 0:30], lambda h: T.ans[:, h:30:2])
+    for o, m, b in (("ok1", 1.0, 0.0), ("ok2", 2.0, 0.0), ("ok3", 2.0, 1.0)):
+        k_ok = ts([k_okp], T[o][:], T.b7[:, 0:24], m, OP.mult, b, OP.add)
     k_am = cp([k_pa], T.am[:], T.b2[:, 0:30])
     wait("g", [k_am])
     spread(lambda r: (T.am[:, 5 * r:5 * r + 5], T.aland[:, 5 * own:5 * own + 5]), "arry")
@@ -354,12 +357,18 @@ def rank_program(g, core, T, topo):
     k_mask = cp([k_mk], T.mask[:], T.b7[:, 0:384])
     k_f0 = tt([k_mask, k_ok, ("arrh", 16), k_selfh], T.f0[:], T.hland[:].indirect(T.ok2[:]), T.mask[:], OP.mult)
     k_mn = tt([], T.maskn[:], T.hland[:].indirect(T.ok3[:]), T.mask[:], OP.mult)
-    Y = T.b0[0:8, 0:384]
-    mms([k_f0, k_gs, k_pm], [(Y, T.gs[:], T.f0[:], True, False)])
-    k_f1 = tt([k_mn, ("arry", 16), k_selfy], T.f1[:], T.aland[:].indirect(T.ok1[:]), T.maskn[:], OP.mult)
-    k_y = mms([k_f1], [(Y, T.gs[:], T.f1[:], False, True)])
-    k_ys = cp([k_y], T.ys[0:8, :], Y)
-    dma("s", [k_ys], "yout", T.y[:], T.ys[0:8, :])
+    Y = [b[0:8, 0:128] for b in (T.b0, T.b1, T.b4)]
+    part = [slice(128 * x, 128 * x + 128) for x in range(3)]
+    for x in range(3):
+        mms([k_f0, k_gs, vread[5]], [(Y[x], T.gs[:], T.f0[:, part[x]], True, False)])
+    k_y = []
+    for x in range(3):
+        k = tt([k_mn, ("arry", 16), k_selfy], T.f1[:, part[x]], T.aland[:].indirect(T.ok1[:, 8 * x:8 * x + 8]),
+               T.maskn[:, part[x]], OP.mult)
+        k_y.append(mms([k], [(Y[x], T.gs[:], T.f1[:, part[x]], False, True)]))
+    for x in range(3):
+        k = cp([k_y[x]], T.ys[0:8, part[x]], Y[x])
+        dma("sas"[x], [k], "y%d" % x, T.y[:, part[x]], T.ys[0:8, part[x]])
 
     cnt.update({"arr1": 16, "arrt": 8, "arra": 8, "arrh": 16, "arry": 16})
     wait("g", [(n, cnt[n]) for n in SEMAPHORES])

from concourse.bass import DstId, RemoteDMATransfer
from concourse.mybir import AluOpType, AxisListType, ActivationFunctionType

OP = AluOpType
COPY = ActivationFunctionType.Copy
NR = 6
NL, NE = 30, 480
V, A = 6144, 2048
BW = 6160
BIG = 2097152.0
SPLIT = 16
BC, VC = 2576, 2048

SHAPES = {
    "float32": "ones_f 160 qrow 6 krow 30 imod 128 sm 36 idn 160 ide 160 ido 160 par 1 npar 1 p7 1 m8 8 gs 8 ownf 3 own5 3 pm 18 "
               "iif 3 kf 3 keyf 3 tf 3 lh0 128 lh1 128 lh2 128 rh0 60 rh1 60 rh2 60 sb 60 vtr 384 atf 128 seed 512 aw 2056 "
               "vw 6152 p2 2048 land 60 tl 30 tland 30 mm 30 ma 30 nh 180 gt 180 hit 180 d1 180 sc 180 rv 480 xv 480 hm 60 "
               "x0 15 x1 15 tb 30 ra 480 xa 480 h1 30 g1 30 h2 30 p1 30 q2 30 q3 30 ans 30 am 30 hland 60 aland 30 "
               "mask 384 maskn 384 f0 384 f1 384 ys 384",
    "int32": "kin 3 tin 3 kidx 1 pari 1 p7i 1 owni 3 posi 3 kki 3 iii 3 keyi 3 nvp 384 nvt 384 nhd 128 nap 128 nat 128",
    "bfloat16": "ones_b 384 tri 128 dsel 576 w1 128 sel0 384 sel1 384 sel2 384 oh 18 lb0 128 lb1 128 lb2 128 rw 24 vph 384 "
                "vpl 384 vth 384 vtm 384 vtl 384 hdh 128 hdl 128 aph 128 apl 128 bw 6160 cw 2048 rr 2880",
    "uint16": "ok1 24 ok2 24 ok3 24 aoff 128 areq 30 asend 30 voff 30 offs 192",
}
SCRATCH = {"b%d" % i: ("psum", [128, 512], "float32") for i in range(8)}
for _d in SHAPES:
    _w = SHAPES[_d].split()
    for _n, _c in zip(_w[::2], _w[1::2]):
        SCRATCH[_n] = ("sbuf", [128, int(_c)], _d)

SEMAPHORES = ("sv sa st sg arr1 arrt arra arrh arry loc self1 selfh selfy y0 y1 y2 ld_kin ld_tin ld_nvp ld_nvt ld_nhd ld_nap "
              "ld_nat row_vph row_vpl row_vth row_vtm row_vtl row_hdh row_hdl row_aph row_apl row_atf row_av row_vv row_at2 "
              "row_av2").split()


def rank_program(g, core, T, topo):
    rank = T.rank_of(core)
    if rank is None:
        return
    Q = {"v": g.vector, "a": g.scalar, "t": g.tensor, "g": g, "s": g.sync}
    SN = {"v": "sv", "a": "sa", "t": "st", "g": "sg"}
    cnt = {}
    seen = {q: {} for q in Q}

    def wait(q, toks):
        for t in toks:
            if t is not None and seen[q].get(t[0], 0) < t[1]:
                Q[q].wait_ge(T.sem[t[0]], t[1])
                seen[q][t[0]] = t[1]

    def done(q, ins):
        ins.then_inc(T.sem[SN[q]], 1)
        cnt[SN[q]] = cnt.get(SN[q], 0) + 1
        return (SN[q], cnt[SN[q]])

    def dma(q, toks, sem, out, in_):
        wait(q, toks)
        Q[q].dma_start(out, in_).then_inc(T.sem[sem], 16)
        cnt[sem] = cnt.get(sem, 0) + 16
        return (sem, cnt[sem])

    def ts(toks, out, in0, s1, op0, s2=None, op1=None):
        wait("v", toks)
        if op1 is None:
            return done("v", g.vector.tensor_scalar(out, in0, s1, None, op0))
        return done("v", g.vector.tensor_scalar(out, in0, s1, s2, op0, op1))

    def tt(toks, out, a, b, op):
        wait("v", toks)
        return done("v", g.vector.tensor_tensor(out, a, b, op))

    def cp(toks, out, in_):
        wait("v", toks)
        return done("v", g.vector.tensor_copy(out, in_))

    def fill(out, c):
        return done("v", g.vector.memset(out, c))

    def act(toks, out, in_, scale=None):
        wait("a", toks)
        if scale is None:
            return done("a", g.scalar.activation(out, in_, COPY))
        return done("a", g.scalar.activation(out, in_, COPY, scale=scale))

    def mms(toks, lst):
        wait("t", toks)
        for x in lst[:-1]:
            g.tensor.matmul(*x)
        return done("t", g.tensor.matmul(*lst[-1]))

    def iota(out, pattern, base, cm):
        return done("g", g.iota(out, pattern, base, cm, allow_small_or_imprecise_dtypes=True))

    def asel(toks, out, in_, pattern, op, base, cm):
        wait("g", toks)
        return done("g", g.affine_select(out, in_, pattern, op, 0.0, base, cm))

    cores = list(T.cores)
    others = [cores[(rank + k) % NR] for k in range(1, NR)]
    nxt = cores[(rank + 1) % NR]

    def pick(dst, first, n):
        return sum(1 << e for e in topo.engines(core, dst)[first:first + n])

    def single(d, out, in_, sem):
        rid, pnc = topo.addr(d)[0], topo.addr(d)[1]
        g.remote_dma(out, in_, T.sem[sem], T.sem["loc"], pnc, rid, pick(d, 0, 8))
        cnt["loc"] = cnt.get("loc", 0) + 8

    def spread(blocks, sem):
        tr = []
        for k, d in enumerate(others[:4]):
            s, o = blocks(T.rank_of(d))
            tr.append(RemoteDMATransfer(dst_ids=[DstId(rid=topo.addr(d)[0], pnc=topo.addr(d)[1])],
                                        dma_engine_mask=pick(d, 2 * k, 2), remote_sem=T.sem[sem], src=s, dst=o))
        g.remote_dma_fused(tr, local_sem=T.sem["loc"])
        cnt["loc"] = cnt.get("loc", 0) + 8
        s, o = blocks(T.rank_of(others[4]))
        single(others[4], o, s, sem)

    ld = {}
    for q, n, src in (("s", "kin", T.rk), ("a", "tin", T.rt), ("s", "nap", T.ap), ("s", "nhd", T.hd), ("s", "nvp", T.vp),
                      ("s", "nvt", T.vt), ("s", "nat", T["at"])):
        ld[n] = dma(q, [], "ld_" + n, T[n][:], src[:])

    k_seed = fill(T.seed[:], BIG)
    k_onesb = fill(T.ones_b[:, 0:128], 1.0)
    k_onesf = fill(T.ones_f[:], 1.0)
    k_bwa = fill(T.bw[:, 0:BC], -BIG)

    def seed(win, c0, c1, scale=None):
        for x in range(c0, c1, 512):
            n = min(512, c1 - x)
            k = act([k_seed], win[:, x:x + n], T.seed[:, 0:n], scale)
        return k

    k_cw = seed(T.cw, 0, 2048, 0.0)
    k_bwb = seed(T.bw, BC, BW, -1.0)
    k_aw = seed(T.aw, 0, 2056)
    k_vwa = seed(T.vw, 0, VC, 0.0)

    k_q = iota(T.qrow[:], [[1, 6]], 0, 0)
    k_tri = asel([k_onesb], T.tri[:], T.ones_b[:, 0:128], [[1, 128]], OP.is_ge, -1, -1)
    k_kr = iota(T.krow[:], [[1, 30]], 0, 0)
    k_im = iota(T.imod[:], [[0, 8], [1, 16]], 0, 0)
    k_kidx = done("g", g.iota(T.kidx[:], [[0, 1]], 0, 1))
    k = asel([k_onesf], T.sm[:], T.ones_f[:, 0:36], [[-3, 4], [-16, 9]], OP.is_ge, 0, 1)
    k = asel([k], T.sm[:, 0:27], T.sm[:, 0:27], [[3, 3], [16, 9]], OP.is_ge, 1, -1)
    k_sm = asel([k], T.sm[:, 27:36], T.sm[:, 27:36], [[16, 9]], OP.is_ge, 11, -1)
    k = asel([k_onesf], T.gs[:], T.ones_f[:, 0:8], [[-16, 8]], OP.is_ge, 0, 1)
    k_gs = asel([k], T.gs[:], T.gs[:], [[16, 8]], OP.is_ge, 15, -1)

    k_own = ts([ld["kin"]], T.owni[:], T.kin[:], 11, OP.arith_shift_right)
    k_ownf = cp([k_own], T.ownf[:], T.owni[:])
    for u in range(3):
        k_oh = ts([k_ownf, k_q], T.oh[:, 6 * u:6 * u + 6], T.qrow[:], T.ownf[:, u:u + 1], OP.is_equal)
    ml = []
    for u in range(3):
        o = T.b0[:, 6 * u:6 * u + 6]
        ml.append((o, T.tri[:], T.oh[:, 6 * u:6 * u + 6], True, u == 0))
        for w in range(u):
            ml.append((o, T.ones_b[:, 0:128], T.oh[:, 6 * w:6 * w + 6], False, w == u - 1))
    k_pos = mms([k_oh, k_tri, k_onesb], ml)
    k_ki = ts([], T.keyi[:], T.kin[:], 2047, OP.bitwise_and)
    cp([ld["tin"]], T.tf[:], T.tin[:])
    ts([], T.own5[:], T.ownf[:], 5.0, OP.mult)
    cp([k_ki], T.keyf[:], T.keyi[:])
    k_pm = tt([k_pos], T.pm[:], T.b0[:, 0:18], T.oh[:], OP.mult)
    for u in range(3):
        wait("v", [k_pm])
        k_po = done("v", g.vector.tensor_reduce(T.posi[:, u:u + 1], T.pm[:, 6 * u:6 * u + 6], AxisListType.X, OP.max))
    k_ii = ts([k_po], T.iii[:], T.posi[:], 15, OP.bitwise_and)
    k_kk = ts([], T.kki[:], T.posi[:], 4, OP.arith_shift_right)
    k_if = cp([k_ii], T.iif[:], T.iii[:])
    k_K = tt([k_kk], T.kf[:], T.kki[:], T.own5[:], OP.add)
    for u in range(3):
        lh, rh = T["lh%d" % u], T["rh%d" % u]
        ts([k_if, k_im], lh[:], T.imod[:], T.iif[:, u:u + 1], OP.is_equal)
        ts([k_K, k_kr], rh[:, 0:60:2], T.krow[:], T.kf[:, u:u + 1], OP.is_equal, T.keyf[:, u:u + 1], OP.mult)
        k_rh = ts([], rh[:, 1:60:2], T.krow[:], T.kf[:, u:u + 1], OP.is_equal, T.tf[:, u:u + 1], OP.mult)
        k_srt = mms([k_rh], [(T.b1[:, 0:60], lh[:], rh[:], u == 0, u == 2)])
    k_sb = cp([k_srt], T.sb[:], T.b1[:, 0:60])
    wait("g", [k_sb])
    spread(lambda q: (T.sb[:, 10 * q:10 * q + 10], T.land[:, 10 * rank:10 * rank + 10]), "arr1")
    k_self1 = dma("s", [k_sb], "self1", T.land[:, 10 * rank:10 * rank + 10], T.sb[:, 10 * rank:10 * rank + 10])

    rw = {}

    def row(n, toks, win, p, c0, src, cols):
        rw[n] = dma("s", toks, "row_" + n, win[p:128:16, c0:c0 + cols], src)

    for n, p in (("ap", 6), ("hd", 3)):
        nat, hi, lo = T["n" + n], T[n + "h"], T[n + "l"]
        k = cp([ld["n" + n]], hi[:], nat[:])
        k2 = tt([k], lo[:], nat[:], hi[:], OP.subtract)
        row(n + "h", [k_cw, k], T.cw, p, 0, hi[:], 2048)
        row(n + "l", [k2], T.cw, p + 1, 0, lo[:], 2048)
    k = cp([ld["nvp"]], T.vph[:], T.nvp[:])
    k2 = tt([k], T.vpl[:], T.nvp[:], T.vph[:], OP.subtract)
    row("vph", [k_bwb, k], T.bw, 0, 8, T.vph[:], V)
    row("vpl", [k2], T.bw, 1, 8, T.vpl[:], V)
    k_dz = fill(T.dsel[:], 0.0)
    k = cp([ld["nvt"]], T.vth[:], T.nvt[:])
    k2 = tt([k], T.vtr[:], T.nvt[:], T.vth[:], OP.subtract)
    k_d = cp([k_sm, k_dz], T.dsel[:, 15:576:16], T.sm[:])
    k3 = cp([k2], T.vtm[:], T.vtr[:])
    k4 = tt([k3], T.vtl[:], T.vtr[:], T.vtm[:], OP.subtract)
    row("vth", [k], T.bw, 9, 8, T.vth[:], V)
    row("vtm", [k3], T.bw, 10, 8, T.vtm[:], V)
    row("vtl", [k4], T.bw, 11, 8, T.vtl[:], V)
    k = cp([ld["nat"]], T.atf[:], T.nat[:])
    row("av", [k_aw], T.aw, 1, 0, T.av[:], A)
    row("atf", [k], T.aw, 0, 0, T.atf[:], A)
    heap_rows = [rw[n] for n in ("vph", "vpl", "vth", "vtm", "vtl")]
    cw_rows = [rw[n] for n in ("aph", "apl", "hdh", "hdl")]

    def wrap(toks, field, out, src):
        x = 144 * field + 15
        return mms(toks, [(out, T.dsel[:, x - r:x - r + 128], src(r), r == 0, r == 15) for r in range(16)])

    k_apw = wrap([k_d] + cw_rows, 2, T.b6[:, 0:128], lambda r: T.cw[:, r:2048:16])

    k_vwb = iota(T.vw[:, VC:6152], [[0, 6152 - VC]], 0, 0)
    k = asel([k_onesb], T.w1[:], T.ones_b[:, 0:128], [[0, 8], [-8, 16]], OP.is_ge, 0, 1)
    k_w1 = asel([k], T.w1[:], T.w1[:], [[0, 8], [8, 16]], OP.is_ge, 7, -1)
    k_idn = asel([k_onesf], T.idn[:], T.ones_f[:], [[1, 160]], OP.is_equal, -16, -1)

    k = ts([k_kidx], T.pari[:], T.kidx[:], 4, OP.arith_shift_right, 1, OP.bitwise_and)
    k2 = ts([], T.p7i[:], T.kidx[:], 7, OP.bitwise_and)
    k_par = cp([k], T.par[:], T.pari[:])
    k_p7 = cp([k2], T.p7[:], T.p7i[:])
    k_ao = cp([k_apw], T.aoff[:], T.b6[:, 0:128])

    EV = 16 * SPLIT

    def gather(win, toks, off, r, x0):
        kb = act(toks, r[:, x0 + EV:x0 + NE], win.indirect(off(SPLIT, NL)))
        wait("v", toks)
        return done("v", g.vector.tensor_copy(r[:, x0:x0 + EV], win.indirect(off(0, SPLIT)))), kb

    def follow(x):
        a, b = 26 * x, min(26 * x + 26, 128)
        return act([k_ao, rw["av"], rw["atf"]], T.p2[:, 16 * a:16 * b], T.aw[:, 0:2056].indirect(T.aoff[:, a:b]))

    k_off = cp([("arr1", 16), k_self1], T.offs[:, 0:30], T.land[:, 0:60:2])
    tread = T.land[:, 1:60:2]
    rtok, nread, vread, ntok, vtok = {}, {}, {}, {}, {}
    rtok[0] = gather(T.cw[:, 0:2048], [k_off] + cw_rows, lambda a, b: T.offs[:, a:b], T.rr, 0)
    follow(0)
    k_tl = cp([], T.tl[:], tread)
    k_np = ts([k_par], T.npar[:], T.par[:], -1.0, OP.mult, 1.0, OP.add)
    k_m8 = ts([k_p7], T.m8[:], T.krow[:, 0:8], T.p7[:], OP.is_equal)
    fill(T.gt[:], 0.0)
    k_gt0 = fill(T.ones_b[:, 128:384], 1.0)
    wait("g", [k_tl])
    single(nxt, T.tland[:], T.tl[:], "arrt")

    nbank = {s: T.b2 if s % 2 else T.b3 for s in range(1, 7)}
    vbank = {s: T.b4 if s % 2 else T.b5 for s in range(1, 6)}

    def later(s):
        x = slice(6 - s, 180, 6)
        k = tt([vtok[s], k_gt0], T.hit[:, x], vbank[s][:, 0:30], tread, OP.is_le)
        vread[s] = tt([], T.gt[:, x], vbank[s][:, 0:30], tread, OP.is_gt)
        return tt([k], T.d1[:, x], T.hit[:, x], T.nh[:, x], OP.mult)

    for s in range(1, 7):
        ntok[s] = wrap(list(rtok[s - 1]) + [nread.get(s - 2)], 1 if s == 1 else 0, nbank[s][:, 0:30],
                       lambda r: T.rr[:, NE * (s - 1) + r:NE * s:16])
        if s > 1:
            vtok[s - 1] = wrap([vread.get(s - 3)], 3, vbank[s - 1][:, 0:30], lambda r: T.rr[:, NE * (s - 1) + r:NE * s:16])
        n = nbank[s][:, 0:30]
        if s == 6:
            break
        x = 32 * s
        k_off = ts([ntok[s]], T.offs[:, x:x + 30], n, 8.0, OP.add, float(V + 8), OP.min)
        rtok[s] = gather(T.bw[:], [k_off] + heap_rows, lambda a, b: T.offs[:, x + a:x + b], T.rr, NE * s)
        if s < 5:
            k_p2 = follow(s)
        cp([], T.nh[:, 6 - s:180:6], n)
        k_mm = cp([], T.mm[:], n) if s == 1 else tt([k_mm], T.mm[:], T.mm[:], n, OP.max)
        nread[s] = k_mm
        for u in range(3):
            if s == 1:
                k_rw = ts([k_m8], T.rw[:, u:24:3], T.m8[:], T.kf[:, u:u + 1], OP.mult)
            if s == 2:
                k_lb = cp([], T["lb%d" % u][:], T["lh%d" % u][:])
        if s > 2:
            later(s - 2)
    k_ma = tt([ntok[6], k_mm], T.ma[:], n, T.mm[:], OP.max)
    k_as = ts([k_ma], T.asend[:], T.ma[:], float(-V), OP.add)
    wait("g", [k_as])
    single(nxt, T.areq[:], T.asend[:], "arra")
    for u in range(3):
        k_sel = asel([k_gt0], T["sel%d" % u][:], T.ones_b[:], [[-1, 8], [1000, 3], [-8, 16]], OP.is_equal, -1000 * u, 1)
    row("vv", [k_vwa, k_vwb], T.vw, 0, 0, T.vv[:], V)
    row("at2", [k_p2], T.aw, 2, 0, T.p2[0:128:16, :], A)
    row("av2", [k_p2], T.aw, 3, 0, T.p2[1:128:16, :], A)

    cp([], T.d1[:, 0:180:6], n)
    later(4)
    k_ide = ts([k_idn, k_np], T.ide[:], T.idn[:], T.npar[:], OP.mult)
    k_ido = ts([], T.ido[:], T.idn[:], T.par[:], OP.mult)
    k_okp = mms([k_rw, k_w1], [(T.b7[:, 0:24], T.w1[:], T.rw[:], True, True)])
    k = later(5)
    wait("v", [k])
    k_sc = done("v", g.vector.tensor_tensor_scan(T.sc[:], T.gt[:], T.d1[:], 0.0, OP.mult, OP.add))
    k_vo = ts([k_sc], T.voff[:], T.sc[:, 5:180:6], float(V), OP.min)

    def turn(toks, src, dst):
        wait("v", toks[:1])
        done("v", g.vector.transpose(dst[:, 0:EV], src[:, 0:EV]))
        wait("v", toks[1:])
        return done("v", g.vector.transpose(dst[:, EV:NE], src[:, EV:NE]))

    def swap(toks, out, src):
        ml = []
        for e in range(2):
            for h in range(2):
                x = 16 + 16 * (e - h)
                ml.append((out[:, e:30:2], (T.ido if e else T.ide)[:, x:x + 128], src(h), h == 0, h == 1))
        return mms(toks, ml)

    k_rv = gather(T.vw[:], [k_vo, rw["vv"]], lambda a, b: T.voff[:, a:b], T.rv, 0)
    k_xv = turn(k_rv, T.rv, T.xv)
    k_pv = swap([k_xv, k_ide, k_ido, k_ao], T.b6[:, 0:30], lambda h: T.xv[:, 16 * h:NE:32])
    k_nf = ts([], T.hm[:, 1:60:2], T.sc[:, 5:180:6], float(V), OP.is_ge)
    ts([("arrt", 8), k_np], T.x0[:], T.tland[:, 0:30:2], T.npar[:], OP.mult)
    k = ts([], T.x1[:], T.tland[:, 1:30:2], T.par[:], OP.mult)
    tt([k], T.tb[:, 0:30:2], T.x0[:], T.x1[:], OP.add)
    k_tb = tt([], T.tb[:, 1:30:2], T.x0[:], T.x1[:], OP.add)

    own = (rank - 1) % NR
    k_ra = gather(T.aw[:, 0:2056], [("arra", 8), rw["at2"], rw["av2"]], lambda a, b: T.areq[:, a:b], T.ra, 0)
    k_hm = cp([k_pv], T.hm[:, 0:60:2], T.b6[:, 0:30])
    wait("g", [k_hm])
    spread(lambda r: (T.hm[:, 10 * r:10 * r + 10], T.hland[:, 10 * rank:10 * rank + 10]), "arrh")
    k_selfh = dma("s", [k_hm], "selfh", T.hland[:, 10 * rank:10 * rank + 10], T.hm[:, 10 * rank:10 * rank + 10])
    k_xa = turn(k_ra, T.ra, T.xa)
    t1, v1, t2, v2 = (T.xa[:, j:NE:16] for j in range(4))
    k_h2 = tt([k_xa, k_tb], T.h2[:], t2, T.tb[:], OP.is_le)
    k_g1 = tt([], T.g1[:], t1, T.tb[:], OP.is_gt)
    k_h1 = tt([], T.h1[:], t1, T.tb[:], OP.is_le)
    k_q2 = tt([k_h2], T.q2[:], T.h2[:], v2, OP.mult)
    k_p1 = tt([k_h1], T.p1[:], T.h1[:], v1, OP.mult)
    k_q3 = tt([k_q2, k_g1], T.q3[:], T.q2[:], T.g1[:], OP.mult)
    k_ans = tt([k_q3, k_p1], T.ans[:], T.q3[:], T.p1[:], OP.add)
    k_pa = swap([k_ans], T.b2[:, 0:30], lambda h: T.ans[:, h:30:2])
    for o, m, b in (("ok1", 1.0, 0.0), ("ok2", 2.0, 0.0), ("ok3", 2.0, 1.0)):
        k_ok = ts([k_okp], T[o][:], T.b7[:, 0:24], m, OP.mult, b, OP.add)
    k_am = cp([k_pa], T.am[:], T.b2[:, 0:30])
    wait("g", [k_am])
    spread(lambda r: (T.am[:, 5 * r:5 * r + 5], T.aland[:, 5 * own:5 * own + 5]), "arry")
    k_selfy = dma("s", [k_am], "selfy", T.aland[:, 5 * own:5 * own + 5], T.am[:, 5 * rank:5 * rank + 5])

    k_mk = mms([k_lb, k_sel, k_ok], [(T.b7[:, 0:384], T["lb%d" % u][:], T["sel%d" % u][:], u == 0, u == 2) for u in range(3)])
    k_mask = cp([k_mk], T.mask[:], T.b7[:, 0:384])
    k_f0 = tt([k_mask, k_ok, ("arrh", 16), k_selfh], T.f0[:], T.hland[:].indirect(T.ok2[:]), T.mask[:], OP.mult)
    k_mn = tt([], T.maskn[:], T.hland[:].indirect(T.ok3[:]), T.mask[:], OP.mult)
    Y = [b[0:8, 0:128] for b in (T.b0, T.b1, T.b4)]
    part = [slice(128 * x, 128 * x + 128) for x in range(3)]
    for x in range(3):
        mms([k_f0, k_gs, vread[5]], [(Y[x], T.gs[:], T.f0[:, part[x]], True, False)])
    k_y = []
    for x in range(3):
        k = tt([k_mn, ("arry", 16), k_selfy], T.f1[:, part[x]], T.aland[:].indirect(T.ok1[:, 8 * x:8 * x + 8]),
               T.maskn[:, part[x]], OP.mult)
        k_y.append(mms([k], [(Y[x], T.gs[:], T.f1[:, part[x]], False, True)]))
    for x in range(3):
        k = cp([k_y[x]], T.ys[0:8, part[x]], Y[x])
        dma("sas"[x], [k], "y%d" % x, T.y[:, part[x]], T.ys[0:8, part[x]])

    cnt.update({"arr1": 16, "arrt": 8, "arra": 8, "arrh": 16, "arry": 16})
    wait("g", [(n, cnt[n]) for n in SEMAPHORES])
